import numpy as np
CORES = [6,14,22,30,134,142,150,158]
N = 8
def setup_inputs(rng):
    return {"x1": rng.standard_normal((N, 128, 8), dtype=np.float32), "x2": rng.standard_normal((N, 128, 512), dtype=np.float32), "x3": rng.standard_normal((N, 128, 1), dtype=np.float32), "x4": rng.standard_normal((N, 128, 128), dtype=np.float32)}
def reference(x1, x2, x3, x4):
    out = {}
    s = x1.sum(axis=0, dtype=np.float64).astype(x1.dtype)
    out["y1"] = np.broadcast_to(s, (N,) + s.shape)
    s = x2.sum(axis=0, dtype=np.float64).astype(x2.dtype)
    out["y2"] = np.broadcast_to(s, (N,) + s.shape)
    s = x3.sum(axis=0, dtype=np.float64).astype(x3.dtype)
    out["y3"] = np.broadcast_to(s, (N,) + s.shape)
    s = x4.sum(axis=0, dtype=np.float64).astype(x4.dtype)
    out["y4"] = np.broadcast_to(s, (N,) + s.shape)
    return out

@@ -1,0 +1,94 @@
+from concourse.bass import DstId, RemoteDMATransfer
+
+NA, NB = 64, 16
+
+SCRATCH = {
+    "src_a": ("dram", [8, 128, NA], "float32"),
+    "res_a": ("dram", [8, 128, NA], "float32"),
+    "land_a": ("dram", [8, 128, NA], "float32"),
+    "src_b": ("dram", [9, 128, NB], "float32"),
+    "res_b": ("dram", [9, 128, NB], "float32"),
+    "land_b": ("dram", [8, 128, NB], "float32"),
+}
+SEMAPHORES = ["ld_a", "ld_b", "st", "sent", "got", "in_a", "in_b"]
+
+
+def owners(ranks):
+    a, b = [], []
+    for r in ranks:
+        base = r - r % 8
+        even = (base // 8) % 2 == 0
+        a.append(base + (7 if even else 3))
+        b.append(base + (3 if even else 7))
+    b.append(ranks[0] - ranks[0] % 8 + 2)
+    return a, b
+
+
+def scatter_masks(src, own):
+    on = [o for o in own if o // 8 == src // 8]
+    w = 8 if len(on) <= 1 else 4
+    masks, e, j = [], 0, 0
+    for o in own:
+        if o // 8 == src // 8:
+            masks.append(((1 << w) - 1) << (8 + j * w))
+            j += 1
+        else:
+            masks.append(1 << e)
+            e += 1
+    return masks
+
+
+def bits(m):
+    return bin(m).count("1")
+
+
+def dst(topo, d, core):
+    rid, pid = topo.addr(d, core)
+    return DstId(rid=rid, pnc=pid)
+
+
+def rank_program(g, core, T, topo):
+    ranks = list(T.cores)
+    rank = T.rank_of(core)
+    own_a, own_b = owners(ranks)
+
+    if rank is not None:
+        g.dma_start(out=T.src_a[:], in_=T.x2[:]).then_inc(T.sem.ld_a, 16)
+        g.dma_start(out=T.src_b[0:8], in_=T.x4[:]).then_inc(T.sem.ld_b, 16)
+        g.dma_start(out=T.src_b[8, 0:64, :], in_=T.x1[:]).then_inc(T.sem.ld_b, 16)
+        g.dma_start(out=T.src_b[8, 64:72, :], in_=T.x3[:]).then_inc(T.sem.ld_b, 16)
+        g.dma_start(out=T.src_b[8, 72:128, :], in_=T.x4[0:7, :]).then_inc(T.sem.ld_b, 16)
+        sent = 0
+        for own, src, land, ld, n_ld in ((own_a, T.src_a, T.land_a, T.sem.ld_a, 1), (own_b, T.src_b, T.land_b, T.sem.ld_b, 4)):
+            masks = scatter_masks(core, own)
+            g.wait_ge(ld, 16 * n_ld)
+            g.remote_dma_fused(
+                [RemoteDMATransfer(dst_ids=[dst(topo, o, core)], dma_engine_mask=masks[k], remote_sem=T.sem.got,
+                                   srcs=[src[k]], dsts=[land[rank]], alu_op=0) for k, o in enumerate(own)],
+                local_sem=T.sem.sent)
+            sent += sum(bits(m) for m in masks)
+        g.wait_ge(T.sem.in_a, 8 * len(own_a))
+        g.dma_start(out=T.y2[:], in_=T.res_a[:]).then_inc(T.sem.st, 16)
+        g.wait_ge(T.sem.in_b, 8 * len(own_b))
+        g.dma_start(out=T.y4[:], in_=T.res_b[0:8]).then_inc(T.sem.st, 16)
+        g.dma_start(out=T.y1[:], in_=T.res_b[8, 0:64, :]).then_inc(T.sem.st, 16)
+        g.dma_start(out=T.y3[:], in_=T.res_b[8, 64:72, :]).then_inc(T.sem.st, 16)
+        g.wait_ge(T.sem.sent, sent)
+        g.wait_ge(T.sem.st, 64)
+        return
+
+    for own, land, res, sem in ((own_a, T.land_a, T.res_a, T.sem.in_a), (own_b, T.land_b, T.res_b, T.sem.in_b)):
+        for k, o in enumerate(own):
+            if o != core:
+                continue
+            g.wait_ge(T.sem.got, sum(bits(scatter_masks(r, own)[k]) for r in ranks))
+            pieces = [land[i] for i in range(len(ranks))]
+            far = [r for r in ranks if r // 8 != core // 8]
+            near = [r for r in ranks if r // 8 == core // 8]
+            tr = [RemoteDMATransfer(dst_ids=[dst(topo, r, core) for r in far], dma_engine_mask=0x00FF, remote_sem=sem,
+                                    srcs=pieces, dsts=[res[k] for r in far], alu_op=1)]
+            if near:
+                tr.append(RemoteDMATransfer(dst_ids=[dst(topo, r, core) for r in near], dma_engine_mask=0xFF00,
+                                            remote_sem=sem, srcs=pieces, dsts=[res[k] for r in near], alu_op=1))
+            g.remote_dma_fused(tr, local_sem=T.sem.sent)
+            g.wait_ge(T.sem.sent, 8 * len(tr))

@@ -1,27 +1,14 @@
 from concourse.bass import DstId, RemoteDMATransfer
 
-NA, NB = 64, 16
-
 SCRATCH = {
-    "src_a": ("dram", [8, 128, NA], "float32"),
-    "res_a": ("dram", [8, 128, NA], "float32"),
-    "land_a": ("dram", [8, 128, NA], "float32"),
-    "src_b": ("dram", [9, 128, NB], "float32"),
-    "res_b": ("dram", [9, 128, NB], "float32"),
-    "land_b": ("dram", [8, 128, NB], "float32"),
+    "src_a": ("dram", [16, 128, 32], "float32"),
+    "res_a": ("dram", [16, 128, 32], "float32"),
+    "land_a": ("dram", [8, 128, 32], "float32"),
+    "src_b": ("dram", [1096, 16], "float32"),
+    "res_b": ("dram", [9, 128, 16], "float32"),
+    "land_b": ("dram", [8, 128, 16], "float32"),
 }
-SEMAPHORES = ["ld_a", "ld_b", "st", "sent", "got", "in_a", "in_b"]
-
-
-def owners(ranks):
-    a, b = [], []
-    for r in ranks:
-        base = r - r % 8
-        even = (base // 8) % 2 == 0
-        a.append(base + (7 if even else 3))
-        b.append(base + (3 if even else 7))
-    b.append(ranks[0] - ranks[0] % 8 + 2)
-    return a, b
+SEMAPHORES = ["ld_a1", "ld_a2", "ld_b", "st", "sent", "got", "in_a1", "in_a2", "in_b"]
 
 
 def scatter_masks(src, own):
@@ -50,16 +37,24 @@ def dst(topo, d, core):
 def rank_program(g, core, T, topo):
     ranks = list(T.cores)
     rank = T.rank_of(core)
-    own_a, own_b = owners(ranks)
+    base = [r - r % 8 for r in ranks]
+    groups = [
+        ([b + 3 for b in base], [T.src_a[k] for k in range(8)], [T.res_a[k] for k in range(8)], T.land_a, T.sem.in_a1),
+        ([b + 2 for b in base], [T.src_a[k] for k in range(8, 16)], [T.res_a[k] for k in range(8, 16)], T.land_a,
+         T.sem.in_a2),
+        ([b + 7 for b in base] + [4 * 8 + 7],
+         [T.src_b[128 * k:128 * k + 128, :] for k in range(8)] + [T.src_b[968:1096, :]],
+         [T.res_b[k] for k in range(9)], T.land_b, T.sem.in_b),
+    ]
 
     if rank is not None:
-        g.dma_start(out=T.src_a[:], in_=T.x2[:]).then_inc(T.sem.ld_a, 16)
-        g.dma_start(out=T.src_b[0:8], in_=T.x4[:]).then_inc(T.sem.ld_b, 16)
-        g.dma_start(out=T.src_b[8, 0:64, :], in_=T.x1[:]).then_inc(T.sem.ld_b, 16)
-        g.dma_start(out=T.src_b[8, 64:72, :], in_=T.x3[:]).then_inc(T.sem.ld_b, 16)
-        g.dma_start(out=T.src_b[8, 72:128, :], in_=T.x4[0:7, :]).then_inc(T.sem.ld_b, 16)
+        g.dma_start(out=T.src_a[0:8], in_=T.x2[0:64, :]).then_inc(T.sem.ld_a1, 16)
+        g.dma_start(out=T.src_a[8:16], in_=T.x2[64:128, :]).then_inc(T.sem.ld_a2, 16)
+        g.dma_start(out=T.src_b[0:1024, :], in_=T.x4[:]).then_inc(T.sem.ld_b, 16)
+        g.dma_start(out=T.src_b[1024:1088, :], in_=T.x1[:]).then_inc(T.sem.ld_b, 16)
+        g.dma_start(out=T.src_b[1088:1096, :], in_=T.x3[:]).then_inc(T.sem.ld_b, 16)
         sent = 0
-        for own, src, land, ld, n_ld in ((own_a, T.src_a, T.land_a, T.sem.ld_a, 1), (own_b, T.src_b, T.land_b, T.sem.ld_b, 4)):
+        for (own, src, res, land, sem), (ld, n_ld) in zip(groups, ((T.sem.ld_a1, 1), (T.sem.ld_a2, 1), (T.sem.ld_b, 3))):
             masks = scatter_masks(core, own)
             g.wait_ge(ld, 16 * n_ld)
             g.remote_dma_fused(
@@ -67,17 +62,19 @@ def rank_program(g, core, T, topo):
                                    srcs=[src[k]], dsts=[land[rank]], alu_op=0) for k, o in enumerate(own)],
                 local_sem=T.sem.sent)
             sent += sum(bits(m) for m in masks)
-        g.wait_ge(T.sem.in_a, 8 * len(own_a))
-        g.dma_start(out=T.y2[:], in_=T.res_a[:]).then_inc(T.sem.st, 16)
-        g.wait_ge(T.sem.in_b, 8 * len(own_b))
+        g.wait_ge(T.sem.in_a1, 64)
+        g.dma_start(out=T.y2[0:64, :], in_=T.res_a[0:8]).then_inc(T.sem.st, 16)
+        g.wait_ge(T.sem.in_a2, 64)
+        g.dma_start(out=T.y2[64:128, :], in_=T.res_a[8:16]).then_inc(T.sem.st, 16)
+        g.wait_ge(T.sem.in_b, 72)
         g.dma_start(out=T.y4[:], in_=T.res_b[0:8]).then_inc(T.sem.st, 16)
-        g.dma_start(out=T.y1[:], in_=T.res_b[8, 0:64, :]).then_inc(T.sem.st, 16)
-        g.dma_start(out=T.y3[:], in_=T.res_b[8, 64:72, :]).then_inc(T.sem.st, 16)
+        g.dma_start(out=T.y1[:], in_=T.res_b[8, 56:120, :]).then_inc(T.sem.st, 16)
+        g.dma_start(out=T.y3[:], in_=T.res_b[8, 120:128, :]).then_inc(T.sem.st, 16)
         g.wait_ge(T.sem.sent, sent)
-        g.wait_ge(T.sem.st, 64)
+        g.wait_ge(T.sem.st, 80)
         return
 
-    for own, land, res, sem in ((own_a, T.land_a, T.res_a, T.sem.in_a), (own_b, T.land_b, T.res_b, T.sem.in_b)):
+    for own, src, res, land, sem in groups:
         for k, o in enumerate(own):
             if o != core:
                 continue

@@ -1,14 +1,30 @@
 from concourse.bass import DstId, RemoteDMATransfer
 
-SCRATCH = {
-    "src_a": ("dram", [16, 128, 32], "float32"),
-    "res_a": ("dram", [16, 128, 32], "float32"),
-    "land_a": ("dram", [8, 128, 32], "float32"),
-    "src_b": ("dram", [1096, 16], "float32"),
-    "res_b": ("dram", [9, 128, 16], "float32"),
-    "land_b": ("dram", [8, 128, 16], "float32"),
-}
-SEMAPHORES = ["ld_a1", "ld_a2", "ld_b", "st", "sent", "got", "in_a1", "in_a2", "in_b"]
+WIDTH = {"x1": 8, "x2": 512, "x3": 1, "x4": 128}
+GROUPS = [
+    (32, [("x2", 0, 64)], 3),
+    (32, [("x2", 64, 128)], 2),
+    (16, [("x4", 0, 128), ("x1", 0, 128), ("x3", 0, 128)], 7),
+]
+SPARE = 4 * 8 + 7
+
+
+def rows_of(grp):
+    n, parts, helper = grp
+    return sum((b - a) * WIDTH[x] for x, a, b in parts) // n
+
+
+def slots_of(grp):
+    return (rows_of(grp) + 127) // 128
+
+
+SCRATCH = {}
+SEMAPHORES = ["st", "sent", "got"]
+for i, grp in enumerate(GROUPS):
+    SCRATCH["src%d" % i] = ("dram", [rows_of(grp), grp[0]], "float32")
+    SCRATCH["res%d" % i] = ("dram", [128 * slots_of(grp), grp[0]], "float32")
+    SCRATCH["land%d" % i] = ("dram", [8, 128, grp[0]], "float32")
+    SEMAPHORES += ["ld%d" % i, "in%d" % i]
 
 
 def scatter_masks(src, own):
@@ -37,55 +53,59 @@ def dst(topo, d, core):
 def rank_program(g, core, T, topo):
     ranks = list(T.cores)
     rank = T.rank_of(core)
-    base = [r - r % 8 for r in ranks]
-    groups = [
-        ([b + 3 for b in base], [T.src_a[k] for k in range(8)], [T.res_a[k] for k in range(8)], T.land_a, T.sem.in_a1),
-        ([b + 2 for b in base], [T.src_a[k] for k in range(8, 16)], [T.res_a[k] for k in range(8, 16)], T.land_a,
-         T.sem.in_a2),
-        ([b + 7 for b in base] + [4 * 8 + 7],
-         [T.src_b[128 * k:128 * k + 128, :] for k in range(8)] + [T.src_b[968:1096, :]],
-         [T.res_b[k] for k in range(9)], T.land_b, T.sem.in_b),
-    ]
+    X = {"x1": T.x1, "x2": T.x2, "x3": T.x3, "x4": T.x4}
+    Y = {"x1": T.y1, "x2": T.y2, "x3": T.y3, "x4": T.y4}
+    SRC, RES, LAND = [T.src0, T.src1, T.src2], [T.res0, T.res1, T.res2], [T.land0, T.land1, T.land2]
+    LD, IN = [T.sem.ld0, T.sem.ld1, T.sem.ld2], [T.sem.in0, T.sem.in1, T.sem.in2]
+    owners = [[r - r % 8 + grp[2] for r in ranks] + [SPARE] * (slots_of(grp) - 8) for grp in GROUPS]
 
     if rank is not None:
-        g.dma_start(out=T.src_a[0:8], in_=T.x2[0:64, :]).then_inc(T.sem.ld_a1, 16)
-        g.dma_start(out=T.src_a[8:16], in_=T.x2[64:128, :]).then_inc(T.sem.ld_a2, 16)
-        g.dma_start(out=T.src_b[0:1024, :], in_=T.x4[:]).then_inc(T.sem.ld_b, 16)
-        g.dma_start(out=T.src_b[1024:1088, :], in_=T.x1[:]).then_inc(T.sem.ld_b, 16)
-        g.dma_start(out=T.src_b[1088:1096, :], in_=T.x3[:]).then_inc(T.sem.ld_b, 16)
+        for i, (n, parts, helper) in enumerate(GROUPS):
+            r0 = 0
+            for x, a, b in parts:
+                r1 = r0 + (b - a) * WIDTH[x] // n
+                g.dma_start(out=SRC[i][r0:r1, :], in_=X[x][a:b, :]).then_inc(LD[i], 16)
+                r0 = r1
         sent = 0
-        for (own, src, res, land, sem), (ld, n_ld) in zip(groups, ((T.sem.ld_a1, 1), (T.sem.ld_a2, 1), (T.sem.ld_b, 3))):
-            masks = scatter_masks(core, own)
-            g.wait_ge(ld, 16 * n_ld)
-            g.remote_dma_fused(
-                [RemoteDMATransfer(dst_ids=[dst(topo, o, core)], dma_engine_mask=masks[k], remote_sem=T.sem.got,
-                                   srcs=[src[k]], dsts=[land[rank]], alu_op=0) for k, o in enumerate(own)],
-                local_sem=T.sem.sent)
+        for i, grp in enumerate(GROUPS):
+            masks = scatter_masks(core, owners[i])
+            tr = []
+            for k, o in enumerate(owners[i]):
+                r0 = min(128 * k, rows_of(grp) - 128)
+                tr.append(RemoteDMATransfer(dst_ids=[dst(topo, o, core)], dma_engine_mask=masks[k], remote_sem=T.sem.got,
+                                            srcs=[SRC[i][r0:r0 + 128, :]], dsts=[LAND[i][rank]], alu_op=0))
+            g.wait_ge(LD[i], 16 * len(grp[1]))
+            g.remote_dma_fused(tr, local_sem=T.sem.sent)
             sent += sum(bits(m) for m in masks)
-        g.wait_ge(T.sem.in_a1, 64)
-        g.dma_start(out=T.y2[0:64, :], in_=T.res_a[0:8]).then_inc(T.sem.st, 16)
-        g.wait_ge(T.sem.in_a2, 64)
-        g.dma_start(out=T.y2[64:128, :], in_=T.res_a[8:16]).then_inc(T.sem.st, 16)
-        g.wait_ge(T.sem.in_b, 72)
-        g.dma_start(out=T.y4[:], in_=T.res_b[0:8]).then_inc(T.sem.st, 16)
-        g.dma_start(out=T.y1[:], in_=T.res_b[8, 56:120, :]).then_inc(T.sem.st, 16)
-        g.dma_start(out=T.y3[:], in_=T.res_b[8, 120:128, :]).then_inc(T.sem.st, 16)
+        stores = 0
+        for i, grp in enumerate(GROUPS):
+            n, parts, helper = grp
+            shift = 128 * slots_of(grp) - rows_of(grp)
+            g.wait_ge(IN[i], 8 * slots_of(grp))
+            r0 = 0
+            for x, a, b in parts:
+                r1 = r0 + (b - a) * WIDTH[x] // n
+                s = shift if r0 >= 128 * (slots_of(grp) - 1) else 0
+                g.dma_start(out=Y[x][a:b, :], in_=RES[i][r0 + s:r1 + s, :]).then_inc(T.sem.st, 16)
+                stores += 1
+                r0 = r1
         g.wait_ge(T.sem.sent, sent)
-        g.wait_ge(T.sem.st, 80)
+        g.wait_ge(T.sem.st, 16 * stores)
         return
 
-    for own, src, res, land, sem in groups:
-        for k, o in enumerate(own):
+    for i, grp in enumerate(GROUPS):
+        for k, o in enumerate(owners[i]):
             if o != core:
                 continue
-            g.wait_ge(T.sem.got, sum(bits(scatter_masks(r, own)[k]) for r in ranks))
-            pieces = [land[i] for i in range(len(ranks))]
+            g.wait_ge(T.sem.got, sum(bits(scatter_masks(r, owners[i])[k]) for r in ranks))
+            pieces = [LAND[i][j] for j in range(len(ranks))]
+            out = RES[i][128 * k:128 * k + 128, :]
             far = [r for r in ranks if r // 8 != core // 8]
             near = [r for r in ranks if r // 8 == core // 8]
-            tr = [RemoteDMATransfer(dst_ids=[dst(topo, r, core) for r in far], dma_engine_mask=0x00FF, remote_sem=sem,
-                                    srcs=pieces, dsts=[res[k] for r in far], alu_op=1)]
+            tr = [RemoteDMATransfer(dst_ids=[dst(topo, r, core) for r in far], dma_engine_mask=0x00FF, remote_sem=IN[i],
+                                    srcs=pieces, dsts=[out for r in far], alu_op=1)]
             if near:
                 tr.append(RemoteDMATransfer(dst_ids=[dst(topo, r, core) for r in near], dma_engine_mask=0xFF00,
-                                            remote_sem=sem, srcs=pieces, dsts=[res[k] for r in near], alu_op=1))
+                                            remote_sem=IN[i], srcs=pieces, dsts=[out for r in near], alu_op=1))
             g.remote_dma_fused(tr, local_sem=T.sem.sent)
             g.wait_ge(T.sem.sent, 8 * len(tr))

from concourse.bass import DstId, RemoteDMATransfer

WIDTH = {"x1": 8, "x2": 512, "x3": 1, "x4": 128}
GROUPS = [
    (32, [("x2", 0, 64)], 3),
    (32, [("x2", 64, 128)], 2),
    (16, [("x4", 0, 128), ("x1", 0, 128), ("x3", 0, 128)], 7),
]
SPARE = 4 * 8 + 7


def rows_of(grp):
    n, parts, helper = grp
    return sum((b - a) * WIDTH[x] for x, a, b in parts) // n


def slots_of(grp):
    return (rows_of(grp) + 127) // 128


SCRATCH = {}
SEMAPHORES = ["st", "sent", "got"]
for i, grp in enumerate(GROUPS):
    SCRATCH["src%d" % i] = ("dram", [rows_of(grp), grp[0]], "float32")
    SCRATCH["res%d" % i] = ("dram", [128 * slots_of(grp), grp[0]], "float32")
    SCRATCH["land%d" % i] = ("dram", [8, 128, grp[0]], "float32")
    SEMAPHORES += ["ld%d" % i, "in%d" % i]


def scatter_masks(src, own):
    on = [o for o in own if o // 8 == src // 8]
    w = 8 if len(on) <= 1 else 4
    masks, e, j = [], 0, 0
    for o in own:
        if o // 8 == src // 8:
            masks.append(((1 << w) - 1) << (8 + j * w))
            j += 1
        else:
            masks.append(1 << e)
            e += 1
    return masks


def bits(m):
    return bin(m).count("1")


def dst(topo, d, core):
    rid, pid = topo.addr(d, core)
    return DstId(rid=rid, pnc=pid)


def rank_program(g, core, T, topo):
    ranks = list(T.cores)
    rank = T.rank_of(core)
    X = {"x1": T.x1, "x2": T.x2, "x3": T.x3, "x4": T.x4}
    Y = {"x1": T.y1, "x2": T.y2, "x3": T.y3, "x4": T.y4}
    SRC, RES, LAND = [T.src0, T.src1, T.src2], [T.res0, T.res1, T.res2], [T.land0, T.land1, T.land2]
    LD, IN = [T.sem.ld0, T.sem.ld1, T.sem.ld2], [T.sem.in0, T.sem.in1, T.sem.in2]
    owners = [[r - r % 8 + grp[2] for r in ranks] + [SPARE] * (slots_of(grp) - 8) for grp in GROUPS]

    if rank is not None:
        for i, (n, parts, helper) in enumerate(GROUPS):
            r0 = 0
            for x, a, b in parts:
                r1 = r0 + (b - a) * WIDTH[x] // n
                g.dma_start(out=SRC[i][r0:r1, :], in_=X[x][a:b, :]).then_inc(LD[i], 16)
                r0 = r1
        sent = 0
        for i, grp in enumerate(GROUPS):
            masks = scatter_masks(core, owners[i])
            tr = []
            for k, o in enumerate(owners[i]):
                r0 = min(128 * k, rows_of(grp) - 128)
                tr.append(RemoteDMATransfer(dst_ids=[dst(topo, o, core)], dma_engine_mask=masks[k], remote_sem=T.sem.got,
                                            srcs=[SRC[i][r0:r0 + 128, :]], dsts=[LAND[i][rank]], alu_op=0))
            g.wait_ge(LD[i], 16 * len(grp[1]))
            g.remote_dma_fused(tr, local_sem=T.sem.sent)
            sent += sum(bits(m) for m in masks)
        stores = 0
        for i, grp in enumerate(GROUPS):
            n, parts, helper = grp
            shift = 128 * slots_of(grp) - rows_of(grp)
            g.wait_ge(IN[i], 8 * slots_of(grp))
            r0 = 0
            for x, a, b in parts:
                r1 = r0 + (b - a) * WIDTH[x] // n
                s = shift if r0 >= 128 * (slots_of(grp) - 1) else 0
                g.dma_start(out=Y[x][a:b, :], in_=RES[i][r0 + s:r1 + s, :]).then_inc(T.sem.st, 16)
                stores += 1
                r0 = r1
        g.wait_ge(T.sem.sent, sent)
        g.wait_ge(T.sem.st, 16 * stores)
        return

    for i, grp in enumerate(GROUPS):
        for k, o in enumerate(owners[i]):
            if o != core:
                continue
            g.wait_ge(T.sem.got, sum(bits(scatter_masks(r, owners[i])[k]) for r in ranks))
            pieces = [LAND[i][j] for j in range(len(ranks))]
            out = RES[i][128 * k:128 * k + 128, :]
            far = [r for r in ranks if r // 8 != core // 8]
            near = [r for r in ranks if r // 8 == core // 8]
            tr = [RemoteDMATransfer(dst_ids=[dst(topo, r, core) for r in far], dma_engine_mask=0x00FF, remote_sem=IN[i],
                                    srcs=pieces, dsts=[out for r in far], alu_op=1)]
            if near:
                tr.append(RemoteDMATransfer(dst_ids=[dst(topo, r, core) for r in near], dma_engine_mask=0xFF00,
                                            remote_sem=IN[i], srcs=pieces, dsts=[out for r in near], alu_op=1))
            g.remote_dma_fused(tr, local_sem=T.sem.sent)
            g.wait_ge(T.sem.sent, 8 * len(tr))
